import numpy as np
import ml_dtypes


def mxq(x, axis, fmt="e4m3"):
    dtype, down = {"e4m3": (ml_dtypes.float8_e4m3fn, 7), "e5m2": (ml_dtypes.float8_e5m2, 14)}[fmt]
    v = np.moveaxis(np.asarray(x, np.float32).astype(ml_dtypes.bfloat16).astype(np.float64), axis, -1)
    blocks = v.reshape(v.shape[:-1] + (-1, 32))
    amax = np.abs(blocks).max(-1, keepdims=True)
    byte = np.maximum(np.where(amax > 0, np.frexp(amax)[1] - 1 + 127, 0) - down, 1)
    scale = np.exp2(byte - 127.0)
    codes = (blocks / scale).astype(np.float32).astype(dtype).astype(np.float64)
    return np.moveaxis((codes * scale).reshape(v.shape), -1, axis)


WIDE = False


def mx_kscale(k):
    if not WIDE:
        return np.ones(k)
    levels = np.array([10, -10, 5, -5, 0])
    if k % 512:
        return np.exp2(np.random.permutation(np.resize(levels, k // 32))).repeat(32)
    a = np.empty((k // 512, 16))
    for p in range(k // 512):
        a[p, :8] = np.random.permutation(np.resize(levels, 8))
        for g in range(8):
            far = levels[np.abs(levels - a[p, g]) >= 10]
            a[p, g + 8] = far[np.random.randint(len(far))]
    return np.exp2(a.ravel()).repeat(32)


def f64(x):
    return np.asarray(x).astype(np.float64)


def striped(idx):
    return np.tile(idx.reshape(-1, 16).T, (8, 1)).astype(np.uint16)


def unstriped(offs):
    return offs[:16].T.reshape(-1).astype(np.int64)


E2M1 = np.array([0.0, 0.5, 1.0, 1.5, 2.0, 3.0, 4.0, 6.0, -0.0, -0.5, -1.0, -1.5, -2.0, -3.0, -4.0, -6.0])


def pack_weight(w, fmt):
    k, n = w.shape
    w = f64(np.asarray(w, np.float32).astype(ml_dtypes.bfloat16)).reshape(k // 32, 32, n)
    amax = np.abs(w).max(1)
    if fmt == "e4m3":
        byte = np.frexp(amax)[1] - 1 + 127 - 7
    else:
        mant, ex = np.frexp(amax / 6.0)
        byte = np.where(mant > 0.5, ex, ex - 1) + 127
    byte = np.clip(np.where(amax > 0, byte, 1), 1, 254)
    scaled = (w * np.exp2(127.0 - byte)[:, None, :]).reshape(k, n).astype(np.float32)
    by_word = np.ascontiguousarray(scaled.reshape(k // 512, 128, 4, n).transpose(0, 1, 3, 2))
    if fmt == "e4m3":
        words = by_word.astype(ml_dtypes.float8_e4m3fn).view(np.uint8)
    else:
        c = by_word.astype(ml_dtypes.float4_e2m1fn).view(np.uint8) & 0xF
        words = (c[..., 0::2] | (c[..., 1::2] << 4)).reshape(k // 512, 128, 2 * n)
    return np.ascontiguousarray(words), np.ascontiguousarray(byte.astype(np.uint8).reshape(k // 512, 16, n))


def unpack_weight(words, scales, fmt):
    g, _, n = scales.shape
    words = np.ascontiguousarray(words).reshape(g, 128, n, -1)
    if fmt == "e4m3":
        vals = words.view(ml_dtypes.float8_e4m3fn).astype(np.float64)
    else:
        nib = np.empty((g, 128, n, 4), np.uint8)
        nib[..., 0::2] = words & 0xF
        nib[..., 1::2] = words >> 4
        vals = E2M1[nib]
    vals = vals * np.repeat(np.exp2(scales.astype(np.float64) - 127.0), 8, axis=1)[..., None]
    return vals.transpose(0, 1, 3, 2).reshape(g * 512, n)


def gelu(v):
    return 0.5 * v * (1.0 + np.tanh(np.sqrt(2.0 / np.pi) * (v + 0.044715 * v**3)))


def bf(x):
    return np.asarray(x, np.float32).astype(ml_dtypes.bfloat16)


def planes(Y):
    n, m = Y.shape
    b = f64(bf(Y)).reshape(n // 32, 32, m)
    amax = np.abs(b).max(1)
    byte = np.clip(np.where(amax > 0, np.frexp(amax)[1] - 1 + 127 - 7, 1), 1, 254)
    codes = (b * np.exp2(127.0 - byte)[:, None, :]).reshape(n, m).astype(np.float32).astype(ml_dtypes.float8_e4m3fn).view(np.uint8)
    words = codes.reshape(n // 512, 128, 4, m).transpose(0, 1, 3, 2)
    return np.ascontiguousarray(words), np.ascontiguousarray(byte.astype(np.uint8).reshape(n // 512, 16, m))


K, H, N, T, S, T2, P = 1536, 512, 1024, 2048, 1024, 2048, 1024


def setup_inputs():
    n = np.random.standard_normal
    s = mx_kscale(K)[:, None]
    u = mx_kscale(H)[:, None]
    tab_words, tab_scales = pack_weight(n((K, T)) * s, "e4m3")
    wa_words, wa_scales = pack_weight(0.8 * n((K, H)) / np.sqrt(K) / s, "e2m1")
    wb = 0.8 * n((K, H)) / np.sqrt(K) / s
    size = np.exp(0.8 * n(N))
    wo_words, wo_scales = pack_weight(n((H, N)) / np.sqrt(H) * size[None, :] / u, "e4m3")
    sign = np.where(n(H) > 0, 1.0, -1.0)
    return {
        "tab_words": tab_words, "tab_scales": tab_scales,
        "offs": striped(np.random.permutation(T)[:S]),
        "offs2": striped(np.random.permutation(T2)[:S]),
        "offs3": striped(np.random.permutation(T2)[:P]),
        "wa_words": wa_words, "wa_scales": wa_scales,
        "wb": wb.astype(np.float32),
        "bias": (0.6 * n(H)).astype(np.float32),
        "page0": (0.8 * n((H, T2))).astype(np.float32),
        "wgs": np.exp(0.3 * n((128, S))).astype(np.float32),
        "tscale": np.random.uniform(0.6, 3.0, H).astype(np.float32),
        "toff": n(H).astype(np.float32),
        "gain": (sign * np.random.uniform(0.5, 2.0, H) * u[:, 0]).astype(np.float32),
        "wo_words": wo_words, "wo_scales": wo_scales,
        "disp": (0.4 * n((N, P)) * size[:, None]).astype(np.float32),
    }


def reference(tab_words, tab_scales, offs, offs2, offs3, wa_words, wa_scales, wb, bias,
              page0, wgs, tscale, toff, gain, wo_words, wo_scales, disp):
    v = unpack_weight(tab_words, tab_scales, "e4m3")[:, unstriped(offs)]
    wa = unpack_weight(wa_words, wa_scales, "e2m1")
    wo = unpack_weight(wo_words, wo_scales, "e4m3")
    left = wa.T @ v
    right = mxq(f64(wb), 0, "e4m3").T @ v
    h = left * (right + f64(bias)[:, None])
    page = f64(page0).copy()
    page[:, unstriped(offs2)] = np.tile(f64(wgs), (H // 128, 1)) * h
    x = 1.0 / (1.0 + np.exp(-(f64(tscale)[:, None] * page[:, unstriped(offs3)] + f64(toff)[:, None])))
    e = mxq(f64(gain)[:, None] * x, 0, "e4m3")
    y = (wo.T @ e) + f64(disp)
    words, scales = planes(y)
    return y, words, scales

@@ -1,0 +1,319 @@
+from contextlib import ExitStack
+
+import concourse.mybir as mybir
+
+K, H, N, T, S, T2, M = 1536, 512, 1024, 2048, 1024, 2048, 1024
+FLOPS = 2 * K * H * S * 2 + 2 * H * N * M
+
+F32 = mybir.dt.float32
+BF16 = mybir.dt.bfloat16
+I32 = mybir.dt.int32
+U32 = mybir.dt.uint32
+U16 = mybir.dt.uint16
+U8 = mybir.dt.uint8
+FP8X4 = mybir.dt.float8_e4m3fn_x4
+FP4X4 = mybir.dt.float4_e2m1fn_x4
+ACT = mybir.ActivationFunctionType
+ALU = mybir.AluOpType
+
+P = 128
+PACK = 4
+K_PASS = P * PACK
+PASSES = K // K_PASS
+GROUPS = N // K_PASS
+QUADS = 4
+QUAD = 32
+ROWS = 4
+BANK = 512
+HALVES = S // BANK
+PER_COL = 16
+UNIT = 256
+SPAN = 3 * QUAD + ROWS
+
+
+def tile_list_plan_warp_features_kernel(
+    tc, tab_words, tab_scales, offs, offs2, offs3, wa_words, wa_scales, wb, bias,
+    page0, wgs, tscale, toff, gain, wo_words, wo_scales, disp, out_0, out_1, out_2,
+):
+    nc = tc.nc
+    with ExitStack() as ctx:
+        keep = ctx.enter_context(tc.tile_pool(name="keep", bufs=1))
+        ring = ctx.enter_context(tc.tile_pool(name="ring", bufs=2))
+        psum = ctx.enter_context(tc.psum_pool(name="psum", bufs=8))
+
+        def held(shape, dtype, name):
+            return keep.tile(shape, dtype, name=name, align_bytes=64)
+
+        def big(name, tag):
+            return keep.tile([P, PACK, K_PASS], F32, name=name, tag=tag, align_bytes=64)
+
+        tab_w = [held([P, T], I32, f"tab_w{a}") for a in range(PASSES)]
+        tab_s = held([P, T], U8, "tab_s")
+        wa_s_raw = held([P, PASSES, H], U8, "wa_s_raw")
+        wo_s_raw = held([P, N], U8, "wo_s_raw")
+        v_s_moved = [held([P, S], U8, f"v_s_moved{a}") for a in range(1, PASSES)]
+        nc.vector.memset(tab_s[:].bitcast(I32), 0)
+        nc.vector.memset(wa_s_raw[:].bitcast(I32), 0)
+        for plane in v_s_moved:
+            nc.vector.memset(plane[:].bitcast(I32), 0)
+        nc.vector.memset(wo_s_raw[:].bitcast(I32), 0)
+
+        for q in range(QUADS):
+            nc.gpsimd.dma_start(
+                out=tab_s[QUAD * q : QUAD * q + PASSES * ROWS, :].bitcast(I32),
+                in_=tab_scales[:, ROWS * q : ROWS * (q + 1), :].bitcast(I32),
+            )
+        for q in range(QUADS):
+            nc.gpsimd.dma_start(
+                out=wa_s_raw[QUAD * q : QUAD * q + ROWS, :, :].bitcast(I32),
+                in_=wa_scales[:, ROWS * q : ROWS * (q + 1), :].rearrange("a r c -> r a c").bitcast(I32),
+            )
+
+        idx = held([P, S // PER_COL], U16, "idx")
+        idx2 = held([P, S // PER_COL], U16, "idx2")
+        idx3 = held([P, M // PER_COL], U16, "idx3")
+        wa_raw = held([P, PASSES, 2 * H], U8, "wa_raw")
+        wb_raw = [big(f"wb_raw{a}", f"big{a}") for a in range(PASSES)]
+
+        def load_tab(a):
+            nc.sync.dma_start(out=tab_w[a][:], in_=tab_words[a].rearrange("p n t -> p (n t)").bitcast(I32))
+
+        def load_wb(a):
+            nc.sync.dma_start(
+                out=wb_raw[a][:], in_=wb[K_PASS * a : K_PASS * (a + 1), :].rearrange("(p j) c -> p j c", j=PACK)
+            )
+
+        load_tab(0)
+        nc.sync.dma_start(idx[:], offs)
+        load_tab(1)
+        nc.sync.dma_start(out=wa_raw[:].bitcast(I32), in_=wa_words.rearrange("a p c -> p a c").bitcast(I32))
+        load_wb(0)
+        load_tab(2)
+        load_wb(1)
+        load_wb(2)
+
+        def load_rows(vec, name):
+            col = held([P, PACK], F32, name)
+            nc.sync.dma_start(out=col[:], in_=vec.rearrange("(p t) -> p t", t=PACK))
+            return col
+
+        bias_c = load_rows(bias, "bias_c")
+        wgs_rows = wgs.rearrange("(q t) j -> q t j", t=PACK)
+        wgs_first = held([P, 1, S], F32, "wgs_first")
+        wgs_rest = held([P, PACK - 1, S], F32, "wgs_rest")
+        for q in range(QUADS):
+            nc.sync.dma_start(out=wgs_first[QUAD * q : QUAD * (q + 1)], in_=wgs_rows[:, 0:1, :])
+        page = [held([P, T2], F32, f"page{t}") for t in range(PACK)]
+        page_rows = page0.rearrange("(p t) c -> t p c", t=PACK)
+        nc.sync.dma_start(out=page[0][:], in_=page_rows[0])
+        nc.sync.dma_start(idx2[:], offs2)
+        for q in range(QUADS):
+            nc.sync.dma_start(out=wgs_rest[QUAD * q : QUAD * (q + 1)], in_=wgs_rows[:, 1:PACK, :])
+        nc.sync.dma_start(out=page[1][:], in_=page_rows[1])
+        nc.sync.dma_start(idx3[:], offs3)
+        tscale_c = load_rows(tscale, "tscale_c")
+        toff_c = load_rows(toff, "toff_c")
+        gain_c = load_rows(gain, "gain_c")
+        nc.sync.dma_start(out=page[2][:], in_=page_rows[2])
+        wo_raw = held([P, N], I32, "wo_raw")
+        nc.sync.dma_start(out=wo_raw[:], in_=wo_words[0].rearrange("p n t -> p (n t)").bitcast(I32))
+        for q in range(QUADS):
+            nc.sync.dma_start(
+                out=wo_s_raw[QUAD * q : QUAD * q + ROWS, :].bitcast(I32),
+                in_=wo_scales[0, ROWS * q : ROWS * (q + 1), :].bitcast(I32),
+            )
+        nc.sync.dma_start(out=page[3][:], in_=page_rows[3])
+        wgs_t = [wgs_first[:, 0, :]] + [wgs_rest[:, t - 1, :] for t in range(1, PACK)]
+
+        v_w = [held([P, S], U32, f"v_w{a}") for a in range(PASSES)]
+        v_s = held([P, S], U8, "v_s")
+
+        def gather_words(a):
+            nc.vector.tensor_copy(v_w[a][:], tab_w[a][:].bitcast(U32).indirect(idx[:]))
+
+        gather_words(0)
+        nc.vector.tensor_copy(v_s[:], tab_s[:].indirect(idx[:]))
+        for a in range(1, PASSES):
+            nc.gpsimd.dma_start(
+                out=v_s_moved[a - 1][0:SPAN, :].bitcast(I32),
+                in_=v_s[ROWS * a : ROWS * a + SPAN, :].bitcast(I32),
+            )
+        gather_words(1)
+        wa_s = held([P, PASSES, H], U8, "wa_s")
+        nc.vector.tensor_copy(
+            out=wa_s[:].rearrange("p a (t q) -> p a q t", t=PACK),
+            in_=wa_s_raw[:].rearrange("p a (q t) -> p a q t", t=PACK),
+        )
+        gather_words(2)
+        wa_w = held([P, PASSES, 2 * H], U8, "wa_w")
+        nc.scalar.copy(
+            out=wa_w[:].bitcast(U16).rearrange("p a (t q) -> p a q t", t=PACK),
+            in_=wa_raw[:].bitcast(U16).rearrange("p a (q t) -> p a q t", t=PACK),
+        )
+
+        PAIR = 2
+        wb_w = [[held([P, PAIR * P], U32, f"wb_w{a}_{u}") for u in range(PACK // PAIR)] for a in range(PASSES)]
+        wb_s = [[held([P, PAIR * P], U8, f"wb_s{a}_{u}") for u in range(PACK // PAIR)] for a in range(PASSES)]
+
+        def quantize_wb(a, u, copy):
+            grouped = keep.tile([P, PAIR, P, PACK], BF16, name=f"wb_bf{a}_{u}", align_bytes=64)
+            copy(
+                out=grouped[:].rearrange("p t q j -> p q j t"),
+                in_=wb_raw[a][:].rearrange("p j (q t) -> p q j t", t=PACK)[:, :, :, PAIR * u : PAIR * (u + 1)],
+            )
+            nc.vector.quantize_mx(
+                out=wb_w[a][u][:].bitcast(FP8X4),
+                scales=wb_s[a][u][:],
+                in_=grouped[:].rearrange("p t q j -> p (t q j)"),
+            )
+
+        quantize_wb(0, 0, nc.scalar.copy)
+        quantize_wb(0, 1, nc.scalar.copy)
+        quantize_wb(1, 0, nc.vector.tensor_copy)
+        quantize_wb(1, 1, nc.scalar.copy)
+        quantize_wb(2, 0, nc.vector.tensor_copy)
+        quantize_wb(2, 1, nc.scalar.copy)
+
+        y = {}
+        for half in range(HALVES):
+            for g in range(GROUPS):
+                i = half * GROUPS + g
+                y[g, half] = big(f"y{i}", f"big{i}")
+                nc.sync.dma_start(
+                    out=y[g, half][:],
+                    in_=disp[K_PASS * g : K_PASS * (g + 1), BANK * half : BANK * (half + 1)].rearrange(
+                        "(p t) m -> p t m", t=PACK
+                    ),
+                )
+
+        def left_sum(t, half):
+            cols = slice(BANK * half, BANK * (half + 1))
+            acc = psum.tile([P, BANK], F32, name="acc")
+            for a in range(PASSES):
+                plane = v_s if a == 0 else v_s_moved[a - 1]
+                nc.tensor.matmul_mx(
+                    out=acc[:],
+                    lhsT=wa_w[:, a, 2 * P * t : 2 * P * (t + 1)].bitcast(FP4X4),
+                    lhsT_scale=wa_s[:, a, P * t : P * (t + 1)],
+                    rhs=v_w[a][:, cols].bitcast(FP8X4),
+                    rhs_scale=plane[:, cols],
+                    start=(a == 0),
+                    stop=(a == PASSES - 1),
+                )
+            left = keep.tile([P, BANK], F32, name=f"left{t}_{half}", align_bytes=64)
+            nc.scalar.copy(out=left[:], in_=acc[:])
+            return left
+
+        def right_sum(t, half):
+            cols = slice(BANK * half, BANK * (half + 1))
+            u, r = divmod(t, PAIR)
+            acc = psum.tile([P, BANK], F32, name="acc")
+            for a in range(PASSES):
+                nc.tensor.matmul_mx(
+                    out=acc[:],
+                    lhsT=wb_w[a][u][:, P * r : P * (r + 1)].bitcast(FP8X4),
+                    lhsT_scale=wb_s[a][u][:, P * r : P * (r + 1)],
+                    rhs=v_w[a][:, cols].bitcast(FP8X4),
+                    rhs_scale=v_s[ROWS * a : P, cols],
+                    start=(a == 0),
+                    stop=(a == PASSES - 1),
+                )
+            return acc
+
+        e_bf = [held([P, BANK, PACK], BF16, f"e_bf{half}") for half in range(HALVES)]
+        wo_w = held([P, GROUPS, PACK, P], U32, "wo_w")
+        wo_s = held([P, GROUPS, PACK, P], U8, "wo_s")
+        last = PACK - 1
+        for t in range(PACK):
+            h = ring.tile([P, S], F32, name="h", align_bytes=64)
+            for half in range(HALVES):
+                left = left_sum(t, half)
+                right = right_sum(t, half)
+                nc.vector.scalar_tensor_tensor(
+                    out=h[:, BANK * half : BANK * (half + 1)],
+                    in0=right[:], scalar=bias_c[:, t : t + 1], in1=left[:], op0=ALU.add, op1=ALU.mult,
+                )
+            nc.vector.tensor_tensor(page[t][:].indirect(idx2[:]), h[:], wgs_t[t], ALU.mult)
+            if t < last:
+                x = ring.tile([P, M], F32, name="x", align_bytes=64)
+                nc.scalar.activation(
+                    out=x[:], in_=page[t][:].indirect(idx3[:]), func=ACT.Sigmoid,
+                    bias=toff_c[:, t : t + 1], scale=tscale_c[:, t : t + 1],
+                )
+                for half in range(HALVES):
+                    nc.scalar.activation(
+                        out=e_bf[half][:, :, t], in_=x[:, BANK * half : BANK * (half + 1)],
+                        func=ACT.Copy, scale=gain_c[:, t : t + 1],
+                    )
+            if t == 1:
+                nc.scalar.copy(
+                    out=wo_w[:].rearrange("p g t q -> p g q t"),
+                    in_=wo_raw[:].bitcast(U32).rearrange("p (g q t) -> p g q t", g=GROUPS, t=PACK),
+                )
+                nc.vector.tensor_copy(
+                    out=wo_s[:].rearrange("p g t q -> p g q t"),
+                    in_=wo_s_raw[:].rearrange("p (g q t) -> p g q t", g=GROUPS, t=PACK),
+                )
+
+        e_w, e_s = [], []
+        for half in range(HALVES):
+            x = keep.tile([P, BANK], F32, name=f"x_last{half}", align_bytes=64)
+            cols16 = slice(BANK // PER_COL * half, BANK // PER_COL * (half + 1))
+            nc.scalar.activation(
+                out=x[:], in_=page[last][:].indirect(idx3[:, cols16]), func=ACT.Sigmoid,
+                bias=toff_c[:, last : last + 1], scale=tscale_c[:, last : last + 1],
+            )
+            nc.vector.tensor_scalar(
+                out=e_bf[half][:, :, last], in0=x[:], scalar1=gain_c[:, last : last + 1], scalar2=None, op0=ALU.mult
+            )
+            e_w.append(held([P, BANK], U32, f"e_w{half}"))
+            e_s.append(held([P, BANK], U8, f"e_s{half}"))
+            nc.vector.quantize_mx(
+                out=e_w[half][:].bitcast(FP8X4), scales=e_s[half][:], in_=e_bf[half][:].rearrange("p m t -> p (m t)")
+            )
+
+        y_s = held([P, GROUPS, M], U8, "y_s")
+        for half in range(HALVES):
+            for g in range(GROUPS):
+                y_w = keep.tile([P, BANK], I32, name=f"y_w{g}_{half}", align_bytes=64)
+                for part in range(BANK // UNIT):
+                    cols = slice(UNIT * part, UNIT * (part + 1))
+                    m0 = BANK * half + UNIT * part
+                    for u in range(PACK // PAIR):
+                        acc = psum.tile([P, PAIR, UNIT], F32, name="acc")
+                        for r in range(PAIR):
+                            nc.tensor.matmul_mx(
+                                out=acc[:, r, :],
+                                lhsT=wo_w[:, g, PAIR * u + r, :].bitcast(FP8X4),
+                                lhsT_scale=wo_s[:, g, PAIR * u + r, :],
+                                rhs=e_w[half][:, cols].bitcast(FP8X4),
+                                rhs_scale=e_s[half][:, cols],
+                                start=True,
+                                stop=True,
+                            )
+                        rows = y[g, half][:, PAIR * u : PAIR * (u + 1), cols]
+                        nc.vector.tensor_tensor(out=rows, in0=acc[:], in1=rows, op=ALU.add)
+                    nc.sync.dma_start(
+                        out=out_0[K_PASS * g : K_PASS * (g + 1), m0 : m0 + UNIT].rearrange("(p t) m -> p t m", t=PACK),
+                        in_=y[g, half][:, :, cols],
+                    )
+                    y_bf = ring.tile([P, UNIT, PACK], BF16, name="y_bf", align_bytes=64)
+                    nc.scalar.copy(
+                        out=y_bf[:].rearrange("p (c i) t -> p c t i", i=4),
+                        in_=y[g, half][:, :, cols].rearrange("p t (c i) -> p c t i", i=4),
+                    )
+                    nc.vector.quantize_mx(
+                        out=y_w[:, cols].bitcast(FP8X4),
+                        scales=y_s[:, g, m0 : m0 + UNIT],
+                        in_=y_bf[:].rearrange("p m t -> p (m t)"),
+                    )
+                nc.sync.dma_start(
+                    out=out_1[g].rearrange("p m t -> p (m t)").bitcast(I32)[:, BANK * half : BANK * (half + 1)],
+                    in_=y_w[:],
+                )
+        for q in range(QUADS):
+            queue = nc.sync if q % 2 == 0 else nc.scalar
+            queue.dma_start(
+                out=out_2[:, ROWS * q : ROWS * (q + 1), :].rearrange("g r m -> r g m").bitcast(I32),
+                in_=y_s[QUAD * q : QUAD * q + ROWS, :, :].bitcast(I32),
+            )

@@ -22,13 +22,20 @@ K_PASS = P * PACK
 PASSES = K // K_PASS
 GROUPS = N // K_PASS
 QUADS = 4
-QUAD = 32
+QUAD = P // QUADS
 ROWS = 4
 BANK = 512
+BANKS = 8
 HALVES = S // BANK
 PER_COL = 16
-UNIT = 256
-SPAN = 3 * QUAD + ROWS
+PAIR = 2
+PART = BANK // PAIR
+LINE = 4
+UNUSED = QUAD - PASSES * ROWS
+SPAN = (QUADS - 1) * QUAD + ROWS
+LEFT_BANK = (0, 2, 2, 2)
+RIGHT_BANK = (2, 4, 4, 4)
+FREE_BANK = 6
 
 
 def tile_list_plan_warp_features_kernel(
@@ -39,30 +46,23 @@ def tile_list_plan_warp_features_kernel(
     with ExitStack() as ctx:
         keep = ctx.enter_context(tc.tile_pool(name="keep", bufs=1))
         ring = ctx.enter_context(tc.tile_pool(name="ring", bufs=2))
-        psum = ctx.enter_context(tc.psum_pool(name="psum", bufs=8))
+        psum = ctx.enter_context(tc.psum_pool(name="psum", bufs=1))
 
-        def held(shape, dtype, name):
-            return keep.tile(shape, dtype, name=name, align_bytes=64)
-
-        def big(name, tag):
-            return keep.tile([P, PACK, K_PASS], F32, name=name, tag=tag, align_bytes=64)
+        def held(shape, dtype, name, tag=None):
+            return keep.tile(shape, dtype, name=name, tag=tag or name, align_bytes=64)
 
         tab_w = [held([P, T], I32, f"tab_w{a}") for a in range(PASSES)]
         tab_s = held([P, T], U8, "tab_s")
         wa_s_raw = held([P, PASSES, H], U8, "wa_s_raw")
+        v_planes = [held([P, S], U8, f"v_plane{a}") for a in range(PASSES)]
         wo_s_raw = held([P, N], U8, "wo_s_raw")
-        v_s_moved = [held([P, S], U8, f"v_s_moved{a}") for a in range(1, PASSES)]
-        nc.vector.memset(tab_s[:].bitcast(I32), 0)
-        nc.vector.memset(wa_s_raw[:].bitcast(I32), 0)
-        for plane in v_s_moved:
+        nc.gpsimd.memset(wa_s_raw[:].bitcast(I32), 0)
+        for q in range(QUADS):
+            nc.vector.memset(tab_s[QUAD * q : QUAD * q + UNUSED, :].bitcast(I32), 0)
+        for plane in v_planes:
             nc.vector.memset(plane[:].bitcast(I32), 0)
         nc.vector.memset(wo_s_raw[:].bitcast(I32), 0)
 
-        for q in range(QUADS):
-            nc.gpsimd.dma_start(
-                out=tab_s[QUAD * q : QUAD * q + PASSES * ROWS, :].bitcast(I32),
-                in_=tab_scales[:, ROWS * q : ROWS * (q + 1), :].bitcast(I32),
-            )
         for q in range(QUADS):
             nc.gpsimd.dma_start(
                 out=wa_s_raw[QUAD * q : QUAD * q + ROWS, :, :].bitcast(I32),
@@ -73,7 +73,7 @@ def tile_list_plan_warp_features_kernel(
         idx2 = held([P, S // PER_COL], U16, "idx2")
         idx3 = held([P, M // PER_COL], U16, "idx3")
         wa_raw = held([P, PASSES, 2 * H], U8, "wa_raw")
-        wb_raw = [big(f"wb_raw{a}", f"big{a}") for a in range(PASSES)]
+        wb_raw = [held([P, PACK, H], F32, f"wb_raw{a}", f"wide{a}") for a in range(PASSES)]
 
         def load_tab(a):
             nc.sync.dma_start(out=tab_w[a][:], in_=tab_words[a].rearrange("p n t -> p (n t)").bitcast(I32))
@@ -83,38 +83,39 @@ def tile_list_plan_warp_features_kernel(
                 out=wb_raw[a][:], in_=wb[K_PASS * a : K_PASS * (a + 1), :].rearrange("(p j) c -> p j c", j=PACK)
             )
 
-        load_tab(0)
-        nc.sync.dma_start(idx[:], offs)
-        load_tab(1)
-        nc.sync.dma_start(out=wa_raw[:].bitcast(I32), in_=wa_words.rearrange("a p c -> p a c").bitcast(I32))
-        load_wb(0)
-        load_tab(2)
-        load_wb(1)
-        load_wb(2)
-
-        def load_rows(vec, name):
+        def load_row_values(vec, name):
             col = held([P, PACK], F32, name)
             nc.sync.dma_start(out=col[:], in_=vec.rearrange("(p t) -> p t", t=PACK))
             return col
 
-        bias_c = load_rows(bias, "bias_c")
-        wgs_rows = wgs.rearrange("(q t) j -> q t j", t=PACK)
-        wgs_first = held([P, 1, S], F32, "wgs_first")
-        wgs_rest = held([P, PACK - 1, S], F32, "wgs_rest")
+        nc.sync.dma_start(idx[:], offs)
+        load_tab(0)
+        load_tab(1)
         for q in range(QUADS):
-            nc.sync.dma_start(out=wgs_first[QUAD * q : QUAD * (q + 1)], in_=wgs_rows[:, 0:1, :])
-        page = [held([P, T2], F32, f"page{t}") for t in range(PACK)]
-        page_rows = page0.rearrange("(p t) c -> t p c", t=PACK)
-        nc.sync.dma_start(out=page[0][:], in_=page_rows[0])
+            nc.sync.dma_start(
+                out=tab_s[QUAD * q + UNUSED : QUAD * (q + 1), :].bitcast(I32),
+                in_=tab_scales[:, ROWS * q : ROWS * (q + 1), :].bitcast(I32),
+            )
+        load_wb(0)
+        nc.sync.dma_start(out=wa_raw[:].bitcast(I32), in_=wa_words.rearrange("a p c -> p a c").bitcast(I32))
+        load_tab(2)
+        load_wb(1)
+        load_wb(2)
+        bias_c = load_row_values(bias, "bias_c")
         nc.sync.dma_start(idx2[:], offs2)
-        for q in range(QUADS):
-            nc.sync.dma_start(out=wgs_rest[QUAD * q : QUAD * (q + 1)], in_=wgs_rows[:, 1:PACK, :])
-        nc.sync.dma_start(out=page[1][:], in_=page_rows[1])
         nc.sync.dma_start(idx3[:], offs3)
-        tscale_c = load_rows(tscale, "tscale_c")
-        toff_c = load_rows(toff, "toff_c")
-        gain_c = load_rows(gain, "gain_c")
-        nc.sync.dma_start(out=page[2][:], in_=page_rows[2])
+        tscale_c = load_row_values(tscale, "tscale_c")
+        toff_c = load_row_values(toff, "toff_c")
+        page_rows = page0.rearrange("(p t) c -> t p c", t=PACK)
+        wgs_rows = wgs.rearrange("(i t) j -> t i j", t=PACK)
+        page = [held([P, T2], F32, f"page{t}") for t in range(PACK)]
+        wgs_t = [held([P, S], F32, f"wgs{t}") for t in range(PACK)]
+        for t in range(PACK):
+            nc.sync.dma_start(out=page[t][:], in_=page_rows[t])
+            for q in range(QUADS):
+                nc.sync.dma_start(out=wgs_t[t][QUAD * q : QUAD * (q + 1), :], in_=wgs_rows[t])
+            if t == 0:
+                gain_c = load_row_values(gain, "gain_c")
         wo_raw = held([P, N], I32, "wo_raw")
         nc.sync.dma_start(out=wo_raw[:], in_=wo_words[0].rearrange("p n t -> p (n t)").bitcast(I32))
         for q in range(QUADS):
@@ -122,10 +123,8 @@ def tile_list_plan_warp_features_kernel(
                 out=wo_s_raw[QUAD * q : QUAD * q + ROWS, :].bitcast(I32),
                 in_=wo_scales[0, ROWS * q : ROWS * (q + 1), :].bitcast(I32),
             )
-        nc.sync.dma_start(out=page[3][:], in_=page_rows[3])
-        wgs_t = [wgs_first[:, 0, :]] + [wgs_rest[:, t - 1, :] for t in range(1, PACK)]
 
-        v_w = [held([P, S], U32, f"v_w{a}") for a in range(PASSES)]
+        v_w = [held([P, S], U32, f"v_w{a}", "tab_s" if a == 1 else None) for a in range(PASSES)]
         v_s = held([P, S], U8, "v_s")
 
         def gather_words(a):
@@ -133,52 +132,45 @@ def tile_list_plan_warp_features_kernel(
 
         gather_words(0)
         nc.vector.tensor_copy(v_s[:], tab_s[:].indirect(idx[:]))
-        for a in range(1, PASSES):
+        for a in range(PASSES):
             nc.gpsimd.dma_start(
-                out=v_s_moved[a - 1][0:SPAN, :].bitcast(I32),
-                in_=v_s[ROWS * a : ROWS * a + SPAN, :].bitcast(I32),
+                out=v_planes[a][0:SPAN, :].bitcast(I32),
+                in_=v_s[UNUSED + ROWS * a : UNUSED + ROWS * a + SPAN, :].bitcast(I32),
             )
         gather_words(1)
-        wa_s = held([P, PASSES, H], U8, "wa_s")
-        nc.vector.tensor_copy(
-            out=wa_s[:].rearrange("p a (t q) -> p a q t", t=PACK),
-            in_=wa_s_raw[:].rearrange("p a (q t) -> p a q t", t=PACK),
-        )
         gather_words(2)
+
+        wa_s = held([P, PASSES, H], U8, "wa_s", f"tab_w{PASSES - 1}")
+        nc.vector.tensor_copy(
+            out=wa_s[:].rearrange("p a (t c) -> p a t c", t=PACK),
+            in_=wa_s_raw[:].rearrange("p a (c t) -> p a t c", t=PACK),
+        )
         wa_w = held([P, PASSES, 2 * H], U8, "wa_w")
         nc.scalar.copy(
-            out=wa_w[:].bitcast(U16).rearrange("p a (t q) -> p a q t", t=PACK),
-            in_=wa_raw[:].bitcast(U16).rearrange("p a (q t) -> p a q t", t=PACK),
+            out=wa_w[:].bitcast(U16).rearrange("p a (t c) -> p a t c", t=PACK),
+            in_=wa_raw[:].bitcast(U16).rearrange("p a (c t) -> p a t c", t=PACK),
         )
 
-        PAIR = 2
         wb_w = [[held([P, PAIR * P], U32, f"wb_w{a}_{u}") for u in range(PACK // PAIR)] for a in range(PASSES)]
         wb_s = [[held([P, PAIR * P], U8, f"wb_s{a}_{u}") for u in range(PACK // PAIR)] for a in range(PASSES)]
-
-        def quantize_wb(a, u, copy):
-            grouped = keep.tile([P, PAIR, P, PACK], BF16, name=f"wb_bf{a}_{u}", align_bytes=64)
-            copy(
-                out=grouped[:].rearrange("p t q j -> p q j t"),
-                in_=wb_raw[a][:].rearrange("p j (q t) -> p q j t", t=PACK)[:, :, :, PAIR * u : PAIR * (u + 1)],
-            )
-            nc.vector.quantize_mx(
-                out=wb_w[a][u][:].bitcast(FP8X4),
-                scales=wb_s[a][u][:],
-                in_=grouped[:].rearrange("p t q j -> p (t q j)"),
-            )
-
-        quantize_wb(0, 0, nc.scalar.copy)
-        quantize_wb(0, 1, nc.scalar.copy)
-        quantize_wb(1, 0, nc.vector.tensor_copy)
-        quantize_wb(1, 1, nc.scalar.copy)
-        quantize_wb(2, 0, nc.vector.tensor_copy)
-        quantize_wb(2, 1, nc.scalar.copy)
+        for a in range(PASSES):
+            for u in range(PACK // PAIR):
+                copy = nc.vector.tensor_copy if (a, u) == (PASSES - 1, 0) else nc.scalar.copy
+                grouped = held([P, PAIR, P, PACK], BF16, f"wb_bf{a}_{u}")
+                copy(
+                    out=grouped[:].rearrange("p t c j -> p c t j"),
+                    in_=wb_raw[a][:].rearrange("p j (c t) -> p c t j", t=PACK)[:, :, PAIR * u : PAIR * (u + 1), :],
+                )
+                nc.vector.quantize_mx(
+                    out=wb_w[a][u][:].bitcast(FP8X4),
+                    scales=wb_s[a][u][:],
+                    in_=grouped[:].rearrange("p t c j -> p (t c j)"),
+                )
 
         y = {}
         for half in range(HALVES):
             for g in range(GROUPS):
-                i = half * GROUPS + g
-                y[g, half] = big(f"y{i}", f"big{i}")
+                y[g, half] = held([P, PACK, BANK], F32, f"y{g}_{half}", f"wide{half * GROUPS + g}")
                 nc.sync.dma_start(
                     out=y[g, half][:],
                     in_=disp[K_PASS * g : K_PASS * (g + 1), BANK * half : BANK * (half + 1)].rearrange(
@@ -188,33 +180,32 @@ def tile_list_plan_warp_features_kernel(
 
         def left_sum(t, half):
             cols = slice(BANK * half, BANK * (half + 1))
-            acc = psum.tile([P, BANK], F32, name="acc")
+            acc = psum.tile([P, BANK], F32, name="left_acc", tag=f"bank{LEFT_BANK[t] + half}")
             for a in range(PASSES):
-                plane = v_s if a == 0 else v_s_moved[a - 1]
                 nc.tensor.matmul_mx(
                     out=acc[:],
                     lhsT=wa_w[:, a, 2 * P * t : 2 * P * (t + 1)].bitcast(FP4X4),
                     lhsT_scale=wa_s[:, a, P * t : P * (t + 1)],
                     rhs=v_w[a][:, cols].bitcast(FP8X4),
-                    rhs_scale=plane[:, cols],
+                    rhs_scale=v_planes[a][:, cols],
                     start=(a == 0),
                     stop=(a == PASSES - 1),
                 )
-            left = keep.tile([P, BANK], F32, name=f"left{t}_{half}", align_bytes=64)
+            left = held([P, BANK], F32, f"left{t}_{half}")
             nc.scalar.copy(out=left[:], in_=acc[:])
             return left
 
         def right_sum(t, half):
             cols = slice(BANK * half, BANK * (half + 1))
-            u, r = divmod(t, PAIR)
-            acc = psum.tile([P, BANK], F32, name="acc")
+            u, member = divmod(t, PAIR)
+            acc = psum.tile([P, BANK], F32, name="right_acc", tag=f"bank{RIGHT_BANK[t] + half}")
             for a in range(PASSES):
                 nc.tensor.matmul_mx(
                     out=acc[:],
-                    lhsT=wb_w[a][u][:, P * r : P * (r + 1)].bitcast(FP8X4),
-                    lhsT_scale=wb_s[a][u][:, P * r : P * (r + 1)],
+                    lhsT=wb_w[a][u][:, P * member : P * (member + 1)].bitcast(FP8X4),
+                    lhsT_scale=wb_s[a][u][:, P * member : P * (member + 1)],
                     rhs=v_w[a][:, cols].bitcast(FP8X4),
-                    rhs_scale=v_s[ROWS * a : P, cols],
+                    rhs_scale=v_planes[a][:, cols],
                     start=(a == 0),
                     stop=(a == PASSES - 1),
                 )
@@ -222,10 +213,9 @@ def tile_list_plan_warp_features_kernel(
 
         e_bf = [held([P, BANK, PACK], BF16, f"e_bf{half}") for half in range(HALVES)]
         wo_w = held([P, GROUPS, PACK, P], U32, "wo_w")
-        wo_s = held([P, GROUPS, PACK, P], U8, "wo_s")
         last = PACK - 1
         for t in range(PACK):
-            h = ring.tile([P, S], F32, name="h", align_bytes=64)
+            h = held([P, S], F32, f"h{t}", "h")
             for half in range(HALVES):
                 left = left_sum(t, half)
                 right = right_sum(t, half)
@@ -233,7 +223,7 @@ def tile_list_plan_warp_features_kernel(
                     out=h[:, BANK * half : BANK * (half + 1)],
                     in0=right[:], scalar=bias_c[:, t : t + 1], in1=left[:], op0=ALU.add, op1=ALU.mult,
                 )
-            nc.vector.tensor_tensor(page[t][:].indirect(idx2[:]), h[:], wgs_t[t], ALU.mult)
+            nc.vector.tensor_tensor(page[t][:].indirect(idx2[:]), h[:], wgs_t[t][:], ALU.mult)
             if t < last:
                 x = ring.tile([P, M], F32, name="x", align_bytes=64)
                 nc.scalar.activation(
@@ -245,22 +235,20 @@ def tile_list_plan_warp_features_kernel(
                         out=e_bf[half][:, :, t], in_=x[:, BANK * half : BANK * (half + 1)],
                         func=ACT.Copy, scale=gain_c[:, t : t + 1],
                     )
-            if t == 1:
+            if t == last - 1:
                 nc.scalar.copy(
-                    out=wo_w[:].rearrange("p g t q -> p g q t"),
-                    in_=wo_raw[:].bitcast(U32).rearrange("p (g q t) -> p g q t", g=GROUPS, t=PACK),
+                    out=wo_w[:].rearrange("p g t (c i) -> p g c t i", i=LINE),
+                    in_=wo_raw[:].bitcast(U32).rearrange("p (g c i t) -> p g c t i", g=GROUPS, t=PACK, i=LINE),
                 )
-                nc.vector.tensor_copy(
-                    out=wo_s[:].rearrange("p g t q -> p g q t"),
-                    in_=wo_s_raw[:].rearrange("p (g q t) -> p g q t", g=GROUPS, t=PACK),
-                )
+        wo_s = held([P, GROUPS, PACK, P], U8, "wo_s", "h")
+        nc.vector.tensor_copy(out=wo_s[:], in_=wo_s_raw[:].rearrange("p (g c t) -> p g t c", g=GROUPS, t=PACK))
 
         e_w, e_s = [], []
         for half in range(HALVES):
-            x = keep.tile([P, BANK], F32, name=f"x_last{half}", align_bytes=64)
-            cols16 = slice(BANK // PER_COL * half, BANK // PER_COL * (half + 1))
+            x = held([P, BANK], F32, f"x_last{half}")
+            entries = slice(BANK // PER_COL * half, BANK // PER_COL * (half + 1))
             nc.scalar.activation(
-                out=x[:], in_=page[last][:].indirect(idx3[:, cols16]), func=ACT.Sigmoid,
+                out=x[:], in_=page[last][:].indirect(idx3[:, entries]), func=ACT.Sigmoid,
                 bias=toff_c[:, last : last + 1], scale=tscale_c[:, last : last + 1],
             )
             nc.vector.tensor_scalar(
@@ -275,17 +263,18 @@ def tile_list_plan_warp_features_kernel(
         y_s = held([P, GROUPS, M], U8, "y_s")
         for half in range(HALVES):
             for g in range(GROUPS):
-                y_w = keep.tile([P, BANK], I32, name=f"y_w{g}_{half}", align_bytes=64)
-                for part in range(BANK // UNIT):
-                    cols = slice(UNIT * part, UNIT * (part + 1))
-                    m0 = BANK * half + UNIT * part
+                y_w = held([P, BANK], I32, f"y_w{g}_{half}")
+                for part in range(BANK // PART):
+                    cols = slice(PART * part, PART * (part + 1))
+                    m0 = BANK * half + PART * part
                     for u in range(PACK // PAIR):
-                        acc = psum.tile([P, PAIR, UNIT], F32, name="acc")
-                        for r in range(PAIR):
+                        bank = (FREE_BANK + PACK * g + PAIR * part + u) % BANKS
+                        acc = psum.tile([P, PAIR, PART], F32, name="acc", tag=f"bank{bank}")
+                        for member in range(PAIR):
                             nc.tensor.matmul_mx(
-                                out=acc[:, r, :],
-                                lhsT=wo_w[:, g, PAIR * u + r, :].bitcast(FP8X4),
-                                lhsT_scale=wo_s[:, g, PAIR * u + r, :],
+                                out=acc[:, member, :],
+                                lhsT=wo_w[:, g, PAIR * u + member, :].bitcast(FP8X4),
+                                lhsT_scale=wo_s[:, g, PAIR * u + member, :],
                                 rhs=e_w[half][:, cols].bitcast(FP8X4),
                                 rhs_scale=e_s[half][:, cols],
                                 start=True,
@@ -294,17 +283,17 @@ def tile_list_plan_warp_features_kernel(
                         rows = y[g, half][:, PAIR * u : PAIR * (u + 1), cols]
                         nc.vector.tensor_tensor(out=rows, in0=acc[:], in1=rows, op=ALU.add)
                     nc.sync.dma_start(
-                        out=out_0[K_PASS * g : K_PASS * (g + 1), m0 : m0 + UNIT].rearrange("(p t) m -> p t m", t=PACK),
+                        out=out_0[K_PASS * g : K_PASS * (g + 1), m0 : m0 + PART].rearrange("(p t) m -> p t m", t=PACK),
                         in_=y[g, half][:, :, cols],
                     )
-                    y_bf = ring.tile([P, UNIT, PACK], BF16, name="y_bf", align_bytes=64)
+                    y_bf = ring.tile([P, PART, PACK], BF16, name="y_bf", align_bytes=64)
                     nc.scalar.copy(
-                        out=y_bf[:].rearrange("p (c i) t -> p c t i", i=4),
-                        in_=y[g, half][:, :, cols].rearrange("p t (c i) -> p c t i", i=4),
+                        out=y_bf[:].rearrange("p (c i) t -> p c t i", i=LINE),
+                        in_=y[g, half][:, :, cols].rearrange("p t (c i) -> p c t i", i=LINE),
                     )
                     nc.vector.quantize_mx(
                         out=y_w[:, cols].bitcast(FP8X4),
-                        scales=y_s[:, g, m0 : m0 + UNIT],
+                        scales=y_s[:, g, m0 : m0 + PART],
                         in_=y_bf[:].rearrange("p m t -> p (m t)"),
                     )
                 nc.sync.dma_start(

from contextlib import ExitStack

import concourse.mybir as mybir

K, H, N, T, S, T2, M = 1536, 512, 1024, 2048, 1024, 2048, 1024
FLOPS = 2 * K * H * S * 2 + 2 * H * N * M

F32 = mybir.dt.float32
BF16 = mybir.dt.bfloat16
I32 = mybir.dt.int32
U32 = mybir.dt.uint32
U16 = mybir.dt.uint16
U8 = mybir.dt.uint8
FP8X4 = mybir.dt.float8_e4m3fn_x4
FP4X4 = mybir.dt.float4_e2m1fn_x4
ACT = mybir.ActivationFunctionType
ALU = mybir.AluOpType

P = 128
PACK = 4
K_PASS = P * PACK
PASSES = K // K_PASS
GROUPS = N // K_PASS
QUADS = 4
QUAD = P // QUADS
ROWS = 4
BANK = 512
BANKS = 8
HALVES = S // BANK
PER_COL = 16
PAIR = 2
PART = BANK // PAIR
LINE = 4
UNUSED = QUAD - PASSES * ROWS
SPAN = (QUADS - 1) * QUAD + ROWS
LEFT_BANK = (0, 2, 2, 2)
RIGHT_BANK = (2, 4, 4, 4)
FREE_BANK = 6


def tile_list_plan_warp_features_kernel(
    tc, tab_words, tab_scales, offs, offs2, offs3, wa_words, wa_scales, wb, bias,
    page0, wgs, tscale, toff, gain, wo_words, wo_scales, disp, out_0, out_1, out_2,
):
    nc = tc.nc
    with ExitStack() as ctx:
        keep = ctx.enter_context(tc.tile_pool(name="keep", bufs=1))
        ring = ctx.enter_context(tc.tile_pool(name="ring", bufs=2))
        psum = ctx.enter_context(tc.psum_pool(name="psum", bufs=1))

        def held(shape, dtype, name, tag=None):
            return keep.tile(shape, dtype, name=name, tag=tag or name, align_bytes=64)

        tab_w = [held([P, T], I32, f"tab_w{a}") for a in range(PASSES)]
        tab_s = held([P, T], U8, "tab_s")
        wa_s_raw = held([P, PASSES, H], U8, "wa_s_raw")
        v_planes = [held([P, S], U8, f"v_plane{a}") for a in range(PASSES)]
        wo_s_raw = held([P, N], U8, "wo_s_raw")
        nc.gpsimd.memset(wa_s_raw[:].bitcast(I32), 0)
        for q in range(QUADS):
            nc.vector.memset(tab_s[QUAD * q : QUAD * q + UNUSED, :].bitcast(I32), 0)
        for plane in v_planes:
            nc.vector.memset(plane[:].bitcast(I32), 0)
        nc.vector.memset(wo_s_raw[:].bitcast(I32), 0)

        for q in range(QUADS):
            nc.gpsimd.dma_start(
                out=wa_s_raw[QUAD * q : QUAD * q + ROWS, :, :].bitcast(I32),
                in_=wa_scales[:, ROWS * q : ROWS * (q + 1), :].rearrange("a r c -> r a c").bitcast(I32),
            )

        idx = held([P, S // PER_COL], U16, "idx")
        idx2 = held([P, S // PER_COL], U16, "idx2")
        idx3 = held([P, M // PER_COL], U16, "idx3")
        wa_raw = held([P, PASSES, 2 * H], U8, "wa_raw")
        wb_raw = [held([P, PACK, H], F32, f"wb_raw{a}", f"wide{a}") for a in range(PASSES)]

        def load_tab(a):
            nc.sync.dma_start(out=tab_w[a][:], in_=tab_words[a].rearrange("p n t -> p (n t)").bitcast(I32))

        def load_wb(a):
            nc.sync.dma_start(
                out=wb_raw[a][:], in_=wb[K_PASS * a : K_PASS * (a + 1), :].rearrange("(p j) c -> p j c", j=PACK)
            )

        def load_row_values(vec, name):
            col = held([P, PACK], F32, name)
            nc.sync.dma_start(out=col[:], in_=vec.rearrange("(p t) -> p t", t=PACK))
            return col

        nc.sync.dma_start(idx[:], offs)
        load_tab(0)
        load_tab(1)
        for q in range(QUADS):
            nc.sync.dma_start(
                out=tab_s[QUAD * q + UNUSED : QUAD * (q + 1), :].bitcast(I32),
                in_=tab_scales[:, ROWS * q : ROWS * (q + 1), :].bitcast(I32),
            )
        load_wb(0)
        nc.sync.dma_start(out=wa_raw[:].bitcast(I32), in_=wa_words.rearrange("a p c -> p a c").bitcast(I32))
        load_tab(2)
        load_wb(1)
        load_wb(2)
        bias_c = load_row_values(bias, "bias_c")
        nc.sync.dma_start(idx2[:], offs2)
        nc.sync.dma_start(idx3[:], offs3)
        tscale_c = load_row_values(tscale, "tscale_c")
        toff_c = load_row_values(toff, "toff_c")
        page_rows = page0.rearrange("(p t) c -> t p c", t=PACK)
        wgs_rows = wgs.rearrange("(i t) j -> t i j", t=PACK)
        page = [held([P, T2], F32, f"page{t}") for t in range(PACK)]
        wgs_t = [held([P, S], F32, f"wgs{t}") for t in range(PACK)]
        for t in range(PACK):
            nc.sync.dma_start(out=page[t][:], in_=page_rows[t])
            for q in range(QUADS):
                nc.sync.dma_start(out=wgs_t[t][QUAD * q : QUAD * (q + 1), :], in_=wgs_rows[t])
            if t == 0:
                gain_c = load_row_values(gain, "gain_c")
        wo_raw = held([P, N], I32, "wo_raw")
        nc.sync.dma_start(out=wo_raw[:], in_=wo_words[0].rearrange("p n t -> p (n t)").bitcast(I32))
        for q in range(QUADS):
            nc.sync.dma_start(
                out=wo_s_raw[QUAD * q : QUAD * q + ROWS, :].bitcast(I32),
                in_=wo_scales[0, ROWS * q : ROWS * (q + 1), :].bitcast(I32),
            )

        v_w = [held([P, S], U32, f"v_w{a}", "tab_s" if a == 1 else None) for a in range(PASSES)]
        v_s = held([P, S], U8, "v_s")

        def gather_words(a):
            nc.vector.tensor_copy(v_w[a][:], tab_w[a][:].bitcast(U32).indirect(idx[:]))

        gather_words(0)
        nc.vector.tensor_copy(v_s[:], tab_s[:].indirect(idx[:]))
        for a in range(PASSES):
            nc.gpsimd.dma_start(
                out=v_planes[a][0:SPAN, :].bitcast(I32),
                in_=v_s[UNUSED + ROWS * a : UNUSED + ROWS * a + SPAN, :].bitcast(I32),
            )
        gather_words(1)
        gather_words(2)

        wa_s = held([P, PASSES, H], U8, "wa_s", f"tab_w{PASSES - 1}")
        nc.vector.tensor_copy(
            out=wa_s[:].rearrange("p a (t c) -> p a t c", t=PACK),
            in_=wa_s_raw[:].rearrange("p a (c t) -> p a t c", t=PACK),
        )
        wa_w = held([P, PASSES, 2 * H], U8, "wa_w")
        nc.scalar.copy(
            out=wa_w[:].bitcast(U16).rearrange("p a (t c) -> p a t c", t=PACK),
            in_=wa_raw[:].bitcast(U16).rearrange("p a (c t) -> p a t c", t=PACK),
        )

        wb_w = [[held([P, PAIR * P], U32, f"wb_w{a}_{u}") for u in range(PACK // PAIR)] for a in range(PASSES)]
        wb_s = [[held([P, PAIR * P], U8, f"wb_s{a}_{u}") for u in range(PACK // PAIR)] for a in range(PASSES)]
        for a in range(PASSES):
            for u in range(PACK // PAIR):
                copy = nc.vector.tensor_copy if (a, u) == (PASSES - 1, 0) else nc.scalar.copy
                grouped = held([P, PAIR, P, PACK], BF16, f"wb_bf{a}_{u}")
                copy(
                    out=grouped[:].rearrange("p t c j -> p c t j"),
                    in_=wb_raw[a][:].rearrange("p j (c t) -> p c t j", t=PACK)[:, :, PAIR * u : PAIR * (u + 1), :],
                )
                nc.vector.quantize_mx(
                    out=wb_w[a][u][:].bitcast(FP8X4),
                    scales=wb_s[a][u][:],
                    in_=grouped[:].rearrange("p t c j -> p (t c j)"),
                )

        y = {}
        for half in range(HALVES):
            for g in range(GROUPS):
                y[g, half] = held([P, PACK, BANK], F32, f"y{g}_{half}", f"wide{half * GROUPS + g}")
                nc.sync.dma_start(
                    out=y[g, half][:],
                    in_=disp[K_PASS * g : K_PASS * (g + 1), BANK * half : BANK * (half + 1)].rearrange(
                        "(p t) m -> p t m", t=PACK
                    ),
                )

        def left_sum(t, half):
            cols = slice(BANK * half, BANK * (half + 1))
            acc = psum.tile([P, BANK], F32, name="left_acc", tag=f"bank{LEFT_BANK[t] + half}")
            for a in range(PASSES):
                nc.tensor.matmul_mx(
                    out=acc[:],
                    lhsT=wa_w[:, a, 2 * P * t : 2 * P * (t + 1)].bitcast(FP4X4),
                    lhsT_scale=wa_s[:, a, P * t : P * (t + 1)],
                    rhs=v_w[a][:, cols].bitcast(FP8X4),
                    rhs_scale=v_planes[a][:, cols],
                    start=(a == 0),
                    stop=(a == PASSES - 1),
                )
            left = held([P, BANK], F32, f"left{t}_{half}")
            nc.scalar.copy(out=left[:], in_=acc[:])
            return left

        def right_sum(t, half):
            cols = slice(BANK * half, BANK * (half + 1))
            u, member = divmod(t, PAIR)
            acc = psum.tile([P, BANK], F32, name="right_acc", tag=f"bank{RIGHT_BANK[t] + half}")
            for a in range(PASSES):
                nc.tensor.matmul_mx(
                    out=acc[:],
                    lhsT=wb_w[a][u][:, P * member : P * (member + 1)].bitcast(FP8X4),
                    lhsT_scale=wb_s[a][u][:, P * member : P * (member + 1)],
                    rhs=v_w[a][:, cols].bitcast(FP8X4),
                    rhs_scale=v_planes[a][:, cols],
                    start=(a == 0),
                    stop=(a == PASSES - 1),
                )
            return acc

        e_bf = [held([P, BANK, PACK], BF16, f"e_bf{half}") for half in range(HALVES)]
        wo_w = held([P, GROUPS, PACK, P], U32, "wo_w")
        last = PACK - 1
        for t in range(PACK):
            h = held([P, S], F32, f"h{t}", "h")
            for half in range(HALVES):
                left = left_sum(t, half)
                right = right_sum(t, half)
                nc.vector.scalar_tensor_tensor(
                    out=h[:, BANK * half : BANK * (half + 1)],
                    in0=right[:], scalar=bias_c[:, t : t + 1], in1=left[:], op0=ALU.add, op1=ALU.mult,
                )
            nc.vector.tensor_tensor(page[t][:].indirect(idx2[:]), h[:], wgs_t[t][:], ALU.mult)
            if t < last:
                x = ring.tile([P, M], F32, name="x", align_bytes=64)
                nc.scalar.activation(
                    out=x[:], in_=page[t][:].indirect(idx3[:]), func=ACT.Sigmoid,
                    bias=toff_c[:, t : t + 1], scale=tscale_c[:, t : t + 1],
                )
                for half in range(HALVES):
                    nc.scalar.activation(
                        out=e_bf[half][:, :, t], in_=x[:, BANK * half : BANK * (half + 1)],
                        func=ACT.Copy, scale=gain_c[:, t : t + 1],
                    )
            if t == last - 1:
                nc.scalar.copy(
                    out=wo_w[:].rearrange("p g t (c i) -> p g c t i", i=LINE),
                    in_=wo_raw[:].bitcast(U32).rearrange("p (g c i t) -> p g c t i", g=GROUPS, t=PACK, i=LINE),
                )
        wo_s = held([P, GROUPS, PACK, P], U8, "wo_s", "h")
        nc.vector.tensor_copy(out=wo_s[:], in_=wo_s_raw[:].rearrange("p (g c t) -> p g t c", g=GROUPS, t=PACK))

        e_w, e_s = [], []
        for half in range(HALVES):
            x = held([P, BANK], F32, f"x_last{half}")
            entries = slice(BANK // PER_COL * half, BANK // PER_COL * (half + 1))
            nc.scalar.activation(
                out=x[:], in_=page[last][:].indirect(idx3[:, entries]), func=ACT.Sigmoid,
                bias=toff_c[:, last : last + 1], scale=tscale_c[:, last : last + 1],
            )
            nc.vector.tensor_scalar(
                out=e_bf[half][:, :, last], in0=x[:], scalar1=gain_c[:, last : last + 1], scalar2=None, op0=ALU.mult
            )
            e_w.append(held([P, BANK], U32, f"e_w{half}"))
            e_s.append(held([P, BANK], U8, f"e_s{half}"))
            nc.vector.quantize_mx(
                out=e_w[half][:].bitcast(FP8X4), scales=e_s[half][:], in_=e_bf[half][:].rearrange("p m t -> p (m t)")
            )

        y_s = held([P, GROUPS, M], U8, "y_s")
        for half in range(HALVES):
            for g in range(GROUPS):
                y_w = held([P, BANK], I32, f"y_w{g}_{half}")
                for part in range(BANK // PART):
                    cols = slice(PART * part, PART * (part + 1))
                    m0 = BANK * half + PART * part
                    for u in range(PACK // PAIR):
                        bank = (FREE_BANK + PACK * g + PAIR * part + u) % BANKS
                        acc = psum.tile([P, PAIR, PART], F32, name="acc", tag=f"bank{bank}")
                        for member in range(PAIR):
                            nc.tensor.matmul_mx(
                                out=acc[:, member, :],
                                lhsT=wo_w[:, g, PAIR * u + member, :].bitcast(FP8X4),
                                lhsT_scale=wo_s[:, g, PAIR * u + member, :],
                                rhs=e_w[half][:, cols].bitcast(FP8X4),
                                rhs_scale=e_s[half][:, cols],
                                start=True,
                                stop=True,
                            )
                        rows = y[g, half][:, PAIR * u : PAIR * (u + 1), cols]
                        nc.vector.tensor_tensor(out=rows, in0=acc[:], in1=rows, op=ALU.add)
                    nc.sync.dma_start(
                        out=out_0[K_PASS * g : K_PASS * (g + 1), m0 : m0 + PART].rearrange("(p t) m -> p t m", t=PACK),
                        in_=y[g, half][:, :, cols],
                    )
                    y_bf = ring.tile([P, PART, PACK], BF16, name="y_bf", align_bytes=64)
                    nc.scalar.copy(
                        out=y_bf[:].rearrange("p (c i) t -> p c t i", i=LINE),
                        in_=y[g, half][:, :, cols].rearrange("p t (c i) -> p c t i", i=LINE),
                    )
                    nc.vector.quantize_mx(
                        out=y_w[:, cols].bitcast(FP8X4),
                        scales=y_s[:, g, m0 : m0 + PART],
                        in_=y_bf[:].rearrange("p m t -> p (m t)"),
                    )
                nc.sync.dma_start(
                    out=out_1[g].rearrange("p m t -> p (m t)").bitcast(I32)[:, BANK * half : BANK * (half + 1)],
                    in_=y_w[:],
                )
        for q in range(QUADS):
            queue = nc.sync if q % 2 == 0 else nc.scalar
            queue.dma_start(
                out=out_2[:, ROWS * q : ROWS * (q + 1), :].rearrange("g r m -> r g m").bitcast(I32),
                in_=y_s[QUAD * q : QUAD * q + ROWS, :, :].bitcast(I32),
            )
